import numpy as np, ml_dtypes
CORES = [44,45,46,47,172,173,174,175,300,301,302,303,428,429,430,431]
N = 16
F = 32
B1, B2, LR, EPS = 0.75, 0.875, 2.0, 0.001
def setup_inputs(rng):
    idle = rng.random((128, N * F)) < 0.125; ib = np.stack([idle[:, F * r:F * r + F] for r in range(N)])
    return {"gr": (rng.standard_normal((N, 128, N * F), dtype=np.float32) * ~idle).astype(ml_dtypes.bfloat16), "m": (rng.standard_normal((N, 128, F), dtype=np.float32) * np.where(ib, 0.004, 1.0)).astype(ml_dtypes.bfloat16), "v": np.where(ib, 2e-6 * 50 ** rng.random((N, 128, F)), (0.5 + rng.standard_normal((N, 128, F), dtype=np.float32) ** 2) * N).astype(ml_dtypes.bfloat16), "w": rng.standard_normal((N, 128, F), dtype=np.float32).astype(ml_dtypes.bfloat16)}
def setup_inputs_big(rng):
    d = setup_inputs(rng)
    for k in ("gr", "m", "v", "w"): d[k] = (d[k].astype(np.float32) * 1024.0).astype(d[k].dtype)
    return d
def setup_inputs_small(rng):
    d = setup_inputs(rng)
    for k in ("gr", "m", "v", "w"): d[k] = (d[k].astype(np.float32) * (1 / 1024.0)).astype(d[k].dtype)
    return d
def setup_inputs_apart(rng):
    d = setup_inputs(rng)
    f = (10.0 ** rng.permutation(np.linspace(-1.5, 1.5, N))).astype(np.float32).reshape(N, 1, 1)
    for k in ("gr", "m", "v", "w"): d[k] = (d[k].astype(np.float32) * f).astype(d[k].dtype)
    return d
def reference(gr, m, v, w):
    GR, M, V, W = gr.astype(np.float64), m.astype(np.float64), v.astype(np.float64), w.astype(np.float64)
    s = GR.sum(axis=0)
    sb = np.stack([s[:, F * r:F * r + F] for r in range(N)])
    m2 = B1 * M + (1 - B1) * sb
    v2 = B2 * V + (1 - B2) * sb ** 2
    w2 = W - LR * m2 / (np.sqrt(v2) + EPS)
    return {"y": np.broadcast_to(np.concatenate(list(w2), axis=1).astype(ml_dtypes.bfloat16), (N, 128, N * F)), "mo": m2.astype(ml_dtypes.bfloat16), "vo": v2.astype(ml_dtypes.bfloat16)}

@@ -1,0 +1,203 @@
+import math
+from concourse.bass import DstId, RemoteDMATransfer
+from concourse.mybir import AluOpType, ActivationFunctionType
+
+F = 32
+L = 4
+W = L * F
+B1, B2, LR, EPS = 0.75, 0.875, 2.0, 0.001
+
+SCRATCH = {
+    "grs": ("sbuf", [128, L * W], "bfloat16"),
+    "l1": ("sbuf", [128, L - 1, W], "bfloat16"),
+    "lS": ("sbuf", [128, W], "bfloat16"),
+    "lC": ("sbuf", [128, W], "bfloat16"),
+    "mine": ("sbuf", [128, 3 * F], "bfloat16"),
+    "mvw": ("sbuf", [128, L, 3 * F], "bfloat16"),
+    "ramp": ("sbuf", [128, 128], "bfloat16"),
+    "i1": ("sbuf", [128, 128], "bfloat16"),
+    "i25": ("sbuf", [128, 128], "bfloat16"),
+    "mc": ("sbuf", [128, W], "bfloat16"),
+    "vc": ("sbuf", [128, W], "float32"),
+    "mv": ("sbuf", [128, L, 2 * F], "bfloat16"),
+    "mvl": ("sbuf", [128, 2 * F], "bfloat16"),
+    "d": ("sbuf", [128, W], "bfloat16"),
+    "e": ("sbuf", [128, W], "bfloat16"),
+    "r": ("sbuf", [128, W], "float32"),
+    "ybuf": ("sbuf", [128, L * W], "bfloat16"),
+    "pA": ("psum", [128, 512], "float32"),
+    "pB": ("psum", [128, 512], "float32"),
+    "pC": ("psum", [128, 512], "float32"),
+    "pU": ("psum", [128, 512], "float32"),
+}
+SEMAPHORES = ["ldg", "ldm", "sent", "a1", "aS", "aC", "a4", "sd", "amv", "sIo", "sI", "sV", "sMc", "sA", "sB", "sSq",
+              "sX", "sM", "sD", "sE", "sR", "sU", "sW", "sty", "stm"]
+
+
+def _chips(T, topo):
+    keys, chips = [], []
+    for c in T.cores:
+        k = (topo.host(c), topo.chip(c))
+        if k not in keys:
+            keys.append(k)
+            chips.append([])
+        chips[keys.index(k)].append(c)
+    return chips
+
+
+def _engines(mask):
+    return [e for e in range(mask.bit_length()) if (mask >> e) & 1]
+
+
+def _mask(engines):
+    return sum(1 << e for e in engines)
+
+
+def rank_program(g, core, T, topo):
+    if T.rank_of(core) is None:
+        return
+    S = T.sem
+    chips = _chips(T, topo)
+    h = [k for k in range(len(chips)) if core in chips[k]][0]
+    q = chips[h].index(core)
+    sw = cab = dia = None
+    for k in range(len(chips)):
+        if k == h:
+            continue
+        if topo.same_plane(core, chips[k][q]):
+            sw = k
+        elif topo.may_write(core, chips[k][q]):
+            cab = k
+        else:
+            dia = k
+    home = q == h
+    peers = [c for c in chips[h] if c != core]
+
+    def dst(c):
+        rid, pid = topo.addr(c, core)
+        return DstId(rid=rid, pnc=pid)
+
+    on = _engines(topo.mask(core, peers[0]))
+    off = _engines(topo.mask(core, chips[sw][q]) & topo.mask(core, chips[cab][q]))
+    onl = [e for e in on if e not in off]
+    sent = [0]
+
+    def call(specs):
+        ts = []
+        for cores_, eng, sem, srcs, d in specs:
+            ts.append(RemoteDMATransfer(dst_ids=[dst(c) for c in cores_], dma_engine_mask=_mask(eng), remote_sem=sem,
+                                        srcs=srcs, dsts=[d for _ in cores_], alu_op=1 if len(srcs) > 1 else 0))
+            sent[0] += len(eng)
+        g.remote_dma_fused(ts, local_sem=S.sent)
+
+    def quarter(t, k):
+        return t[:, k * W:(k + 1) * W]
+
+    def pk(a, b):
+        return T.mvw[:, q, a:b] if home else T.mine[:, a:b]
+
+    own = quarter(T.grs, q)
+    yq = quarter(T.ybuf, q)
+    pA, pB, pC, pU = T.pA[:, 0:W], T.pB[:, 0:W], T.pC[:, 0:W], T.pU[:, 0:W]
+    side = 4 * (L - 1) if home else 16
+
+    g.sync.dma_start(T.grs[:], T.gr[:]).then_inc(S.ldg, 16)
+    g.scalar.dma_start(pk(0, F), T.m[:]).then_inc(S.ldm, 16)
+    g.scalar.dma_start(pk(F, 2 * F), T.v[:]).then_inc(S.ldm, 16)
+    g.sync.dma_start(pk(2 * F, 3 * F), T.w[:]).then_inc(S.ldm, 16)
+
+    g.iota(T.ramp[:], [[-1, 128]], 0, 1, allow_small_or_imprecise_dtypes=True).then_inc(S.sIo, 1)
+    g.vector.wait_ge(S.sIo, 1)
+    g.vector.tensor_scalar(T.i1[:], T.ramp[:], 0.0, None, AluOpType.is_equal).then_inc(S.sI, 1)
+    g.vector.tensor_scalar(T.i25[:], T.ramp[:], 0.0, 1.0 - B1, AluOpType.is_equal, AluOpType.mult).then_inc(S.sI, 1)
+
+    g.wait_ge(S.ldg, 16)
+    sets = [onl[0:4], onl[4:8], off[4:8]]
+    specs = []
+    for n, c in enumerate(peers):
+        k = chips[h].index(c)
+        specs.append(([c], sets[n], S.a1, [quarter(T.grs, k)], T.l1[:, q if q < k else q - 1, :]))
+    call(specs)
+    g.wait_ge(S.ldm, 48)
+    slot = T.mvw[:, q, :]
+    specs = [([chips[sw][h]], off[0:4], S.sd, [pk(0, 3 * F)], slot),
+             ([chips[cab][h]], off[4:8], S.sd, [pk(0, 3 * F)], slot)]
+    if not home:
+        specs.append(([chips[h][h]], onl[0:4], S.sd, [pk(0, 3 * F)], slot))
+    call(specs)
+    g.wait_ge(S.a1, 4 * (L - 1))
+    chip_parts = [own] + [T.l1[:, k, :] for k in range(L - 1)]
+    call([([chips[sw][q]], off, S.aS, chip_parts, T.lS[:])])
+    if q == sw:
+        g.wait_ge(S.sd, side)
+        call([([chips[cab][q]], off, S.sd, [T.mvw[:, 0:L // 2, :]], T.mvw[:, 0:L // 2, :])])
+    if q == cab:
+        g.wait_ge(S.sd, side)
+        call([([chips[sw][q]], off, S.sd, [T.mvw[:, L // 2:L, :]], T.mvw[:, L // 2:L, :])])
+    g.wait_ge(S.aS, len(off))
+    call([([chips[cab][q]], off, S.aC, chip_parts + [T.lS[:]], T.lC[:])])
+    if home:
+        g.wait_ge(S.sX, 1)
+        g.wait_ge(S.sM, 1)
+        call([([c], sets[n], S.amv, [T.mv[:, chips[h].index(c), :]], T.mvl[:]) for n, c in enumerate(peers)])
+    g.wait_ge(S.sW, 1)
+    call([(peers, on, S.a4, [yq], yq)])
+
+    pe = g.tensor
+    pe.wait_ge(S.sI, 2)
+    pe.wait_ge(S.ldg, 16)
+    pe.matmul(pA, T.i1[:], own, True, False)
+    pe.matmul(pB, T.i25[:], own, True, False)
+    pe.wait_ge(S.a1, 4 * (L - 1))
+    for k in range(L - 1):
+        pe.matmul(pA, T.i1[:], T.l1[:, k, :], False, False)
+        pe.matmul(pB, T.i25[:], T.l1[:, k, :], False, False)
+    pe.wait_ge(S.aS, len(off))
+    pe.matmul(pA, T.i1[:], T.lS[:], False, False)
+    pe.matmul(pB, T.i25[:], T.lS[:], False, False)
+    pe.wait_ge(S.aC, len(off))
+    pe.matmul(pA, T.i1[:], T.lC[:], False, True).then_inc(S.sA, 1)
+    pe.matmul(pB, T.i25[:], T.lC[:], False, False)
+    pe.wait_ge(S.sMc, 1)
+    pe.matmul(pB, T.i25[:], T.mc[:], False, True).then_inc(S.sB, 1)
+
+    ve = g.vector
+    if home:
+        ve.wait_ge(S.ldm, 48)
+    ve.wait_ge(S.sd, side)
+    ve.tensor_scalar(T.vc[:], T.mvw[:, :, F:2 * F], B2, None, AluOpType.mult).then_inc(S.sV, 1)
+    ve.tensor_scalar(T.mc[:], T.mvw[:, :, 0:F], B1 / (1.0 - B1), None, AluOpType.mult).then_inc(S.sMc, 1)
+    ve.wait_ge(S.sV, 1)
+    ve.wait_ge(S.sSq, 1)
+    ve.tensor_tensor(T.mv[:, :, F:2 * F], pC, T.vc[:], AluOpType.add).then_inc(S.sX, 1)
+    ve.wait_ge(S.sB, 1)
+    if home:
+        ve.tensor_copy(T.mv[:, :, 0:F], pB).then_inc(S.sM, 1)
+    ve.wait_ge(S.sD, 1)
+    ve.tensor_scalar(T.e[:], T.d[:], EPS / LR, None, AluOpType.add).then_inc(S.sE, 1)
+    ve.wait_ge(S.sE, 1)
+    ve.reciprocal(T.r[:], T.e[:]).then_inc(S.sR, 1)
+    ve.wait_ge(S.sR, 1)
+    ve.tensor_tensor(pU, pB, T.r[:], AluOpType.mult).then_inc(S.sU, 1)
+    ve.wait_ge(S.sU, 1)
+    ve.tensor_tensor(yq, T.mvw[:, :, 2 * F:3 * F], pU, AluOpType.subtract).then_inc(S.sW, 1)
+
+    ac = g.scalar
+    ac.wait_ge(S.sA, 1)
+    ac.activation(pC, pA, ActivationFunctionType.Square, scale=math.sqrt(1.0 - B2)).then_inc(S.sSq, 1)
+    ac.wait_ge(S.sX, 1)
+    ac.activation(T.d[:], T.mv[:, :, F:2 * F], ActivationFunctionType.Sqrt, scale=1.0 / (LR * LR)).then_inc(S.sD, 1)
+    if home:
+        ac.wait_ge(S.sM, 1)
+    else:
+        ac.wait_ge(S.amv, 4)
+    ac.dma_start(T.mo[:], T.mv[:, q, 0:F] if home else T.mvl[:, 0:F]).then_inc(S.stm, 16)
+    ac.dma_start(T.vo[:], T.mv[:, q, F:2 * F] if home else T.mvl[:, F:2 * F]).then_inc(S.stm, 16)
+    ac.wait_ge(S.stm, 32)
+
+    g.sync.wait_ge(S.sW, 1)
+    g.sync.wait_ge(S.a4, len(on) * (L - 1))
+    g.sync.dma_start(T.y[:], T.ybuf[:]).then_inc(S.sty, 16)
+    g.sync.wait_ge(S.sty, 16)
+
+    g.wait_ge(S.sent, sent[0])

@@ -109,7 +109,8 @@ def rank_program(g, core, T, topo):
     g.iota(T.ramp[:], [[-1, 128]], 0, 1, allow_small_or_imprecise_dtypes=True).then_inc(S.sIo, 1)
     g.vector.wait_ge(S.sIo, 1)
     g.vector.tensor_scalar(T.i1[:], T.ramp[:], 0.0, None, AluOpType.is_equal).then_inc(S.sI, 1)
-    g.vector.tensor_scalar(T.i25[:], T.ramp[:], 0.0, 1.0 - B1, AluOpType.is_equal, AluOpType.mult).then_inc(S.sI, 1)
+    g.scalar.wait_ge(S.sI, 1)
+    g.scalar.activation(T.i25[:], T.i1[:], ActivationFunctionType.Sqrt, scale=(1.0 - B1) ** 2).then_inc(S.sI, 1)
 
     g.wait_ge(S.ldg, 16)
     sets = [onl[0:4], onl[4:8], off[4:8]]

@@ -2,6 +2,7 @@ import math
 from concourse.bass import DstId, RemoteDMATransfer
 from concourse.mybir import AluOpType, ActivationFunctionType
 
+WORLD = 512
 F = 32
 L = 4
 W = L * F
@@ -13,8 +14,13 @@ SCRATCH = {
     "lS": ("sbuf", [128, W], "bfloat16"),
     "lC": ("sbuf", [128, W], "bfloat16"),
     "mine": ("sbuf", [128, 3 * F], "bfloat16"),
+    "hA": ("sbuf", [128, 3 * F], "bfloat16"),
+    "hB": ("sbuf", [128, 3 * F], "bfloat16"),
+    "cs": ("sbuf", [128, W], "bfloat16"),
     "mvw": ("sbuf", [128, L, 3 * F], "bfloat16"),
     "ramp": ("sbuf", [128, 128], "bfloat16"),
+    "i16s": ("sbuf", [128, 128], "bfloat16"),
+    "i16": ("sbuf", [128, 128], "bfloat16"),
     "i1": ("sbuf", [128, 128], "bfloat16"),
     "i25": ("sbuf", [128, 128], "bfloat16"),
     "mc": ("sbuf", [128, W], "bfloat16"),
@@ -24,14 +30,16 @@ SCRATCH = {
     "d": ("sbuf", [128, W], "bfloat16"),
     "e": ("sbuf", [128, W], "bfloat16"),
     "r": ("sbuf", [128, W], "float32"),
+    "wc": ("sbuf", [128, W], "bfloat16"),
+    "nu": ("sbuf", [128, W], "bfloat16"),
     "ybuf": ("sbuf", [128, L * W], "bfloat16"),
     "pA": ("psum", [128, 512], "float32"),
     "pB": ("psum", [128, 512], "float32"),
     "pC": ("psum", [128, 512], "float32"),
-    "pU": ("psum", [128, 512], "float32"),
+    "pS": ("psum", [128, 512], "float32"),
 }
 SEMAPHORES = ["ldg", "ldm", "sent", "a1", "aS", "aC", "a4", "sd", "amv", "sIo", "sI", "sV", "sMc", "sA", "sB", "sSq",
-              "sX", "sM", "sD", "sE", "sR", "sU", "sW", "sty", "stm"]
+              "sX", "sM", "sD", "sE", "sR", "sU", "sW", "sty", "stm", "pa", "pb", "sS", "sCs", "aI", "aJ", "sIs", "sWc"]
 
 
 def _chips(T, topo):
@@ -45,6 +53,15 @@ def _chips(T, topo):
     return chips
 
 
+def _helpers(chips, topo):
+    out = []
+    for ch in chips:
+        c0 = ch[0]
+        out.append([c for c in range(WORLD) if topo.host(c) == topo.host(c0) and topo.chip(c) == topo.chip(c0)
+                    and topo.die(c) != topo.die(c0)][0:L])
+    return out
+
+
 def _engines(mask):
     return [e for e in range(mask.bit_length()) if (mask >> e) & 1]
 
@@ -54,12 +71,15 @@ def _mask(engines):
 
 
 def rank_program(g, core, T, topo):
-    if T.rank_of(core) is None:
-        return
     S = T.sem
     chips = _chips(T, topo)
-    h = [k for k in range(len(chips)) if core in chips[k]][0]
-    q = chips[h].index(core)
+    helpers = _helpers(chips, topo)
+    helper = T.rank_of(core) is None
+    mine = [k for k in range(len(chips)) if core in chips[k] or core in helpers[k]]
+    if not mine:
+        return
+    h = mine[0]
+    q = helpers[h].index(core) if helper else chips[h].index(core)
     sw = cab = dia = None
     for k in range(len(chips)):
         if k == h:
@@ -70,6 +90,7 @@ def rank_program(g, core, T, topo):
             cab = k
         else:
             dia = k
+    n1, n2 = (sw, cab) if q % 2 == 0 else (cab, sw)
     home = q == h
     peers = [c for c in chips[h] if c != core]
 
@@ -78,7 +99,7 @@ def rank_program(g, core, T, topo):
         return DstId(rid=rid, pnc=pid)
 
     on = _engines(topo.mask(core, peers[0]))
-    off = _engines(topo.mask(core, chips[sw][q]) & topo.mask(core, chips[cab][q]))
+    off = _engines(topo.mask(core, chips[n1][q]) & topo.mask(core, chips[n2][q]))
     onl = [e for e in on if e not in off]
     sent = [0]
 
@@ -90,6 +111,21 @@ def rank_program(g, core, T, topo):
             sent[0] += len(eng)
         g.remote_dma_fused(ts, local_sem=S.sent)
 
+    if helper:
+        g.iota(T.ramp[:], [[-1, 128]], 0, 1, allow_small_or_imprecise_dtypes=True).then_inc(S.sIo, 1)
+        g.vector.wait_ge(S.sIo, 1)
+        g.vector.tensor_scalar(T.i1[:], T.ramp[:], 0.0, None, AluOpType.is_equal).then_inc(S.sI, 1)
+        g.wait_ge(S.sI, 1)
+        call([([chips[h][q]], on, S.aI, [T.i1[:]], T.i1[:])])
+        slot = T.mvw[:, q, :]
+        g.wait_ge(S.pb, 4)
+        g.wait_ge(S.pa, 4)
+        call([([chips[n2][n1]], off[0:4], S.sd, [T.hB[:]], slot),
+              ([chips[n2][h]], off[4:8], S.sd, [T.hA[:]], slot),
+              ([chips[h][n1]], onl[0:4], S.sd, [T.hB[:]], slot)])
+        g.wait_ge(S.sent, sent[0])
+        return
+
     def quarter(t, k):
         return t[:, k * W:(k + 1) * W]
 
@@ -98,8 +134,8 @@ def rank_program(g, core, T, topo):
 
     own = quarter(T.grs, q)
     yq = quarter(T.ybuf, q)
-    pA, pB, pC, pU = T.pA[:, 0:W], T.pB[:, 0:W], T.pC[:, 0:W], T.pU[:, 0:W]
-    side = 4 * (L - 1) if home else 16
+    pA, pB, pC, pS = T.pA[:, 0:W], T.pB[:, 0:W], T.pC[:, 0:W], T.pS[:, 0:W]
+    side = 4 * (L - 1) if home else 4 * L
 
     g.sync.dma_start(T.grs[:], T.gr[:]).then_inc(S.ldg, 16)
     g.scalar.dma_start(pk(0, F), T.m[:]).then_inc(S.ldm, 16)
@@ -108,10 +144,13 @@ def rank_program(g, core, T, topo):
 
     g.iota(T.ramp[:], [[-1, 128]], 0, 1, allow_small_or_imprecise_dtypes=True).then_inc(S.sIo, 1)
     g.vector.wait_ge(S.sIo, 1)
-    g.vector.tensor_scalar(T.i1[:], T.ramp[:], 0.0, None, AluOpType.is_equal).then_inc(S.sI, 1)
-    g.scalar.wait_ge(S.sI, 1)
-    g.scalar.activation(T.i25[:], T.i1[:], ActivationFunctionType.Sqrt, scale=(1.0 - B1) ** 2).then_inc(S.sI, 1)
+    g.vector.tensor_scalar(T.i16s[:], T.ramp[:], 0.0, (1.0 - B1) ** 2, AluOpType.is_equal,
+                           AluOpType.mult).then_inc(S.sIs, 1)
+    g.scalar.wait_ge(S.aJ, len(on))
+    g.scalar.activation(T.i25[:], T.i16[:], ActivationFunctionType.Sqrt).then_inc(S.sI, 1)
 
+    g.wait_ge(S.sIs, 1)
+    call([([chips[h][(q + 1) % L]], on, S.aJ, [T.i16s[:]], T.i16[:])])
     g.wait_ge(S.ldg, 16)
     sets = [onl[0:4], onl[4:8], off[4:8]]
     specs = []
@@ -120,36 +159,36 @@ def rank_program(g, core, T, topo):
         specs.append(([c], sets[n], S.a1, [quarter(T.grs, k)], T.l1[:, q if q < k else q - 1, :]))
     call(specs)
     g.wait_ge(S.ldm, 48)
-    slot = T.mvw[:, q, :]
-    specs = [([chips[sw][h]], off[0:4], S.sd, [pk(0, 3 * F)], slot),
-             ([chips[cab][h]], off[4:8], S.sd, [pk(0, 3 * F)], slot)]
+    specs = [([helpers[n1][q]], off[0:4], S.pb, [pk(0, 3 * F)], T.hB[:]),
+             ([helpers[h][q]], onl[0:4], S.pa, [pk(0, 3 * F)], T.hA[:])]
     if not home:
-        specs.append(([chips[h][h]], onl[0:4], S.sd, [pk(0, 3 * F)], slot))
+        specs.append(([chips[h][h]], onl[4:8], S.sd, [pk(0, 3 * F)], T.mvw[:, q, :]))
     call(specs)
     g.wait_ge(S.a1, 4 * (L - 1))
     chip_parts = [own] + [T.l1[:, k, :] for k in range(L - 1)]
-    call([([chips[sw][q]], off, S.aS, chip_parts, T.lS[:])])
-    if q == sw:
-        g.wait_ge(S.sd, side)
-        call([([chips[cab][q]], off, S.sd, [T.mvw[:, 0:L // 2, :]], T.mvw[:, 0:L // 2, :])])
-    if q == cab:
-        g.wait_ge(S.sd, side)
-        call([([chips[sw][q]], off, S.sd, [T.mvw[:, L // 2:L, :]], T.mvw[:, L // 2:L, :])])
+    call([([chips[n1][q]], off, S.aS, chip_parts, T.lS[:])])
+    g.wait_ge(S.sCs, 1)
     g.wait_ge(S.aS, len(off))
-    call([([chips[cab][q]], off, S.aC, chip_parts + [T.lS[:]], T.lC[:])])
+    call([([chips[n2][q]], off, S.aC, [T.cs[:], T.lS[:]], T.lC[:])])
     if home:
         g.wait_ge(S.sX, 1)
         g.wait_ge(S.sM, 1)
         call([([c], sets[n], S.amv, [T.mv[:, chips[h].index(c), :]], T.mvl[:]) for n, c in enumerate(peers)])
-    g.wait_ge(S.sW, 1)
-    call([(peers, on, S.a4, [yq], yq)])
+    g.wait_ge(S.sWc, 1)
+    g.wait_ge(S.sU, 1)
+    call([(peers, on, S.a4, [T.wc[:], T.nu[:]], yq)])
 
     pe = g.tensor
-    pe.wait_ge(S.sI, 2)
+    pe.wait_ge(S.aI, len(on))
     pe.wait_ge(S.ldg, 16)
+    pe.matmul(pS, T.i1[:], own, True, False)
+    pe.wait_ge(S.sI, 1)
     pe.matmul(pA, T.i1[:], own, True, False)
     pe.matmul(pB, T.i25[:], own, True, False)
     pe.wait_ge(S.a1, 4 * (L - 1))
+    for k in range(L - 2):
+        pe.matmul(pS, T.i1[:], T.l1[:, k, :], False, False)
+    pe.matmul(pS, T.i1[:], T.l1[:, L - 2, :], False, True).then_inc(S.sS, 1)
     for k in range(L - 1):
         pe.matmul(pA, T.i1[:], T.l1[:, k, :], False, False)
         pe.matmul(pB, T.i25[:], T.l1[:, k, :], False, False)
@@ -168,6 +207,7 @@ def rank_program(g, core, T, topo):
     ve.wait_ge(S.sd, side)
     ve.tensor_scalar(T.vc[:], T.mvw[:, :, F:2 * F], B2, None, AluOpType.mult).then_inc(S.sV, 1)
     ve.tensor_scalar(T.mc[:], T.mvw[:, :, 0:F], B1 / (1.0 - B1), None, AluOpType.mult).then_inc(S.sMc, 1)
+    ve.tensor_copy(T.wc[:], T.mvw[:, :, 2 * F:3 * F]).then_inc(S.sWc, 1)
     ve.wait_ge(S.sV, 1)
     ve.wait_ge(S.sSq, 1)
     ve.tensor_tensor(T.mv[:, :, F:2 * F], pC, T.vc[:], AluOpType.add).then_inc(S.sX, 1)
@@ -175,15 +215,18 @@ def rank_program(g, core, T, topo):
     if home:
         ve.tensor_copy(T.mv[:, :, 0:F], pB).then_inc(S.sM, 1)
     ve.wait_ge(S.sD, 1)
-    ve.tensor_scalar(T.e[:], T.d[:], EPS / LR, None, AluOpType.add).then_inc(S.sE, 1)
+    ve.tensor_scalar(T.e[:], T.d[:], -1.0, -EPS / LR, AluOpType.mult, AluOpType.add).then_inc(S.sE, 1)
     ve.wait_ge(S.sE, 1)
     ve.reciprocal(T.r[:], T.e[:]).then_inc(S.sR, 1)
     ve.wait_ge(S.sR, 1)
-    ve.tensor_tensor(pU, pB, T.r[:], AluOpType.mult).then_inc(S.sU, 1)
+    ve.tensor_tensor(T.nu[:], pB, T.r[:], AluOpType.mult).then_inc(S.sU, 1)
     ve.wait_ge(S.sU, 1)
-    ve.tensor_tensor(yq, T.mvw[:, :, 2 * F:3 * F], pU, AluOpType.subtract).then_inc(S.sW, 1)
+    ve.wait_ge(S.sWc, 1)
+    ve.tensor_tensor(yq, T.wc[:], T.nu[:], AluOpType.add).then_inc(S.sW, 1)
 
     ac = g.scalar
+    ac.wait_ge(S.sS, 1)
+    ac.activation(T.cs[:], pS, ActivationFunctionType.Copy).then_inc(S.sCs, 1)
     ac.wait_ge(S.sA, 1)
     ac.activation(pC, pA, ActivationFunctionType.Square, scale=math.sqrt(1.0 - B2)).then_inc(S.sSq, 1)
     ac.wait_ge(S.sX, 1)

import math
from concourse.bass import DstId, RemoteDMATransfer
from concourse.mybir import AluOpType, ActivationFunctionType

WORLD = 512
F = 32
L = 4
W = L * F
B1, B2, LR, EPS = 0.75, 0.875, 2.0, 0.001

SCRATCH = {
    "grs": ("sbuf", [128, L * W], "bfloat16"),
    "l1": ("sbuf", [128, L - 1, W], "bfloat16"),
    "lS": ("sbuf", [128, W], "bfloat16"),
    "lC": ("sbuf", [128, W], "bfloat16"),
    "mine": ("sbuf", [128, 3 * F], "bfloat16"),
    "hA": ("sbuf", [128, 3 * F], "bfloat16"),
    "hB": ("sbuf", [128, 3 * F], "bfloat16"),
    "cs": ("sbuf", [128, W], "bfloat16"),
    "mvw": ("sbuf", [128, L, 3 * F], "bfloat16"),
    "ramp": ("sbuf", [128, 128], "bfloat16"),
    "i16s": ("sbuf", [128, 128], "bfloat16"),
    "i16": ("sbuf", [128, 128], "bfloat16"),
    "i1": ("sbuf", [128, 128], "bfloat16"),
    "i25": ("sbuf", [128, 128], "bfloat16"),
    "mc": ("sbuf", [128, W], "bfloat16"),
    "vc": ("sbuf", [128, W], "float32"),
    "mv": ("sbuf", [128, L, 2 * F], "bfloat16"),
    "mvl": ("sbuf", [128, 2 * F], "bfloat16"),
    "d": ("sbuf", [128, W], "bfloat16"),
    "e": ("sbuf", [128, W], "bfloat16"),
    "r": ("sbuf", [128, W], "float32"),
    "wc": ("sbuf", [128, W], "bfloat16"),
    "nu": ("sbuf", [128, W], "bfloat16"),
    "ybuf": ("sbuf", [128, L * W], "bfloat16"),
    "pA": ("psum", [128, 512], "float32"),
    "pB": ("psum", [128, 512], "float32"),
    "pC": ("psum", [128, 512], "float32"),
    "pS": ("psum", [128, 512], "float32"),
}
SEMAPHORES = ["ldg", "ldm", "sent", "a1", "aS", "aC", "a4", "sd", "amv", "sIo", "sI", "sV", "sMc", "sA", "sB", "sSq",
              "sX", "sM", "sD", "sE", "sR", "sU", "sW", "sty", "stm", "pa", "pb", "sS", "sCs", "aI", "aJ", "sIs", "sWc"]


def _chips(T, topo):
    keys, chips = [], []
    for c in T.cores:
        k = (topo.host(c), topo.chip(c))
        if k not in keys:
            keys.append(k)
            chips.append([])
        chips[keys.index(k)].append(c)
    return chips


def _helpers(chips, topo):
    out = []
    for ch in chips:
        c0 = ch[0]
        out.append([c for c in range(WORLD) if topo.host(c) == topo.host(c0) and topo.chip(c) == topo.chip(c0)
                    and topo.die(c) != topo.die(c0)][0:L])
    return out


def _engines(mask):
    return [e for e in range(mask.bit_length()) if (mask >> e) & 1]


def _mask(engines):
    return sum(1 << e for e in engines)


def rank_program(g, core, T, topo):
    S = T.sem
    chips = _chips(T, topo)
    helpers = _helpers(chips, topo)
    helper = T.rank_of(core) is None
    mine = [k for k in range(len(chips)) if core in chips[k] or core in helpers[k]]
    if not mine:
        return
    h = mine[0]
    q = helpers[h].index(core) if helper else chips[h].index(core)
    sw = cab = dia = None
    for k in range(len(chips)):
        if k == h:
            continue
        if topo.same_plane(core, chips[k][q]):
            sw = k
        elif topo.may_write(core, chips[k][q]):
            cab = k
        else:
            dia = k
    n1, n2 = (sw, cab) if q % 2 == 0 else (cab, sw)
    home = q == h
    peers = [c for c in chips[h] if c != core]

    def dst(c):
        rid, pid = topo.addr(c, core)
        return DstId(rid=rid, pnc=pid)

    on = _engines(topo.mask(core, peers[0]))
    off = _engines(topo.mask(core, chips[n1][q]) & topo.mask(core, chips[n2][q]))
    onl = [e for e in on if e not in off]
    sent = [0]

    def call(specs):
        ts = []
        for cores_, eng, sem, srcs, d in specs:
            ts.append(RemoteDMATransfer(dst_ids=[dst(c) for c in cores_], dma_engine_mask=_mask(eng), remote_sem=sem,
                                        srcs=srcs, dsts=[d for _ in cores_], alu_op=1 if len(srcs) > 1 else 0))
            sent[0] += len(eng)
        g.remote_dma_fused(ts, local_sem=S.sent)

    if helper:
        g.iota(T.ramp[:], [[-1, 128]], 0, 1, allow_small_or_imprecise_dtypes=True).then_inc(S.sIo, 1)
        g.vector.wait_ge(S.sIo, 1)
        g.vector.tensor_scalar(T.i1[:], T.ramp[:], 0.0, None, AluOpType.is_equal).then_inc(S.sI, 1)
        g.wait_ge(S.sI, 1)
        call([([chips[h][q]], on, S.aI, [T.i1[:]], T.i1[:])])
        slot = T.mvw[:, q, :]
        g.wait_ge(S.pb, 4)
        g.wait_ge(S.pa, 4)
        call([([chips[n2][n1]], off[0:4], S.sd, [T.hB[:]], slot),
              ([chips[n2][h]], off[4:8], S.sd, [T.hA[:]], slot),
              ([chips[h][n1]], onl[0:4], S.sd, [T.hB[:]], slot)])
        g.wait_ge(S.sent, sent[0])
        return

    def quarter(t, k):
        return t[:, k * W:(k + 1) * W]

    def pk(a, b):
        return T.mvw[:, q, a:b] if home else T.mine[:, a:b]

    own = quarter(T.grs, q)
    yq = quarter(T.ybuf, q)
    pA, pB, pC, pS = T.pA[:, 0:W], T.pB[:, 0:W], T.pC[:, 0:W], T.pS[:, 0:W]
    side = 4 * (L - 1) if home else 4 * L

    g.sync.dma_start(T.grs[:], T.gr[:]).then_inc(S.ldg, 16)
    g.scalar.dma_start(pk(0, F), T.m[:]).then_inc(S.ldm, 16)
    g.scalar.dma_start(pk(F, 2 * F), T.v[:]).then_inc(S.ldm, 16)
    g.sync.dma_start(pk(2 * F, 3 * F), T.w[:]).then_inc(S.ldm, 16)

    g.iota(T.ramp[:], [[-1, 128]], 0, 1, allow_small_or_imprecise_dtypes=True).then_inc(S.sIo, 1)
    g.vector.wait_ge(S.sIo, 1)
    g.vector.tensor_scalar(T.i16s[:], T.ramp[:], 0.0, (1.0 - B1) ** 2, AluOpType.is_equal,
                           AluOpType.mult).then_inc(S.sIs, 1)
    g.scalar.wait_ge(S.aJ, len(on))
    g.scalar.activation(T.i25[:], T.i16[:], ActivationFunctionType.Sqrt).then_inc(S.sI, 1)

    g.wait_ge(S.sIs, 1)
    call([([chips[h][(q + 1) % L]], on, S.aJ, [T.i16s[:]], T.i16[:])])
    g.wait_ge(S.ldg, 16)
    sets = [onl[0:4], onl[4:8], off[4:8]]
    specs = []
    for n, c in enumerate(peers):
        k = chips[h].index(c)
        specs.append(([c], sets[n], S.a1, [quarter(T.grs, k)], T.l1[:, q if q < k else q - 1, :]))
    call(specs)
    g.wait_ge(S.ldm, 48)
    specs = [([helpers[n1][q]], off[0:4], S.pb, [pk(0, 3 * F)], T.hB[:]),
             ([helpers[h][q]], onl[0:4], S.pa, [pk(0, 3 * F)], T.hA[:])]
    if not home:
        specs.append(([chips[h][h]], onl[4:8], S.sd, [pk(0, 3 * F)], T.mvw[:, q, :]))
    call(specs)
    g.wait_ge(S.a1, 4 * (L - 1))
    chip_parts = [own] + [T.l1[:, k, :] for k in range(L - 1)]
    call([([chips[n1][q]], off, S.aS, chip_parts, T.lS[:])])
    g.wait_ge(S.sCs, 1)
    g.wait_ge(S.aS, len(off))
    call([([chips[n2][q]], off, S.aC, [T.cs[:], T.lS[:]], T.lC[:])])
    if home:
        g.wait_ge(S.sX, 1)
        g.wait_ge(S.sM, 1)
        call([([c], sets[n], S.amv, [T.mv[:, chips[h].index(c), :]], T.mvl[:]) for n, c in enumerate(peers)])
    g.wait_ge(S.sWc, 1)
    g.wait_ge(S.sU, 1)
    call([(peers, on, S.a4, [T.wc[:], T.nu[:]], yq)])

    pe = g.tensor
    pe.wait_ge(S.aI, len(on))
    pe.wait_ge(S.ldg, 16)
    pe.matmul(pS, T.i1[:], own, True, False)
    pe.wait_ge(S.sI, 1)
    pe.matmul(pA, T.i1[:], own, True, False)
    pe.matmul(pB, T.i25[:], own, True, False)
    pe.wait_ge(S.a1, 4 * (L - 1))
    for k in range(L - 2):
        pe.matmul(pS, T.i1[:], T.l1[:, k, :], False, False)
    pe.matmul(pS, T.i1[:], T.l1[:, L - 2, :], False, True).then_inc(S.sS, 1)
    for k in range(L - 1):
        pe.matmul(pA, T.i1[:], T.l1[:, k, :], False, False)
        pe.matmul(pB, T.i25[:], T.l1[:, k, :], False, False)
    pe.wait_ge(S.aS, len(off))
    pe.matmul(pA, T.i1[:], T.lS[:], False, False)
    pe.matmul(pB, T.i25[:], T.lS[:], False, False)
    pe.wait_ge(S.aC, len(off))
    pe.matmul(pA, T.i1[:], T.lC[:], False, True).then_inc(S.sA, 1)
    pe.matmul(pB, T.i25[:], T.lC[:], False, False)
    pe.wait_ge(S.sMc, 1)
    pe.matmul(pB, T.i25[:], T.mc[:], False, True).then_inc(S.sB, 1)

    ve = g.vector
    if home:
        ve.wait_ge(S.ldm, 48)
    ve.wait_ge(S.sd, side)
    ve.tensor_scalar(T.vc[:], T.mvw[:, :, F:2 * F], B2, None, AluOpType.mult).then_inc(S.sV, 1)
    ve.tensor_scalar(T.mc[:], T.mvw[:, :, 0:F], B1 / (1.0 - B1), None, AluOpType.mult).then_inc(S.sMc, 1)
    ve.tensor_copy(T.wc[:], T.mvw[:, :, 2 * F:3 * F]).then_inc(S.sWc, 1)
    ve.wait_ge(S.sV, 1)
    ve.wait_ge(S.sSq, 1)
    ve.tensor_tensor(T.mv[:, :, F:2 * F], pC, T.vc[:], AluOpType.add).then_inc(S.sX, 1)
    ve.wait_ge(S.sB, 1)
    if home:
        ve.tensor_copy(T.mv[:, :, 0:F], pB).then_inc(S.sM, 1)
    ve.wait_ge(S.sD, 1)
    ve.tensor_scalar(T.e[:], T.d[:], -1.0, -EPS / LR, AluOpType.mult, AluOpType.add).then_inc(S.sE, 1)
    ve.wait_ge(S.sE, 1)
    ve.reciprocal(T.r[:], T.e[:]).then_inc(S.sR, 1)
    ve.wait_ge(S.sR, 1)
    ve.tensor_tensor(T.nu[:], pB, T.r[:], AluOpType.mult).then_inc(S.sU, 1)
    ve.wait_ge(S.sU, 1)
    ve.wait_ge(S.sWc, 1)
    ve.tensor_tensor(yq, T.wc[:], T.nu[:], AluOpType.add).then_inc(S.sW, 1)

    ac = g.scalar
    ac.wait_ge(S.sS, 1)
    ac.activation(T.cs[:], pS, ActivationFunctionType.Copy).then_inc(S.sCs, 1)
    ac.wait_ge(S.sA, 1)
    ac.activation(pC, pA, ActivationFunctionType.Square, scale=math.sqrt(1.0 - B2)).then_inc(S.sSq, 1)
    ac.wait_ge(S.sX, 1)
    ac.activation(T.d[:], T.mv[:, :, F:2 * F], ActivationFunctionType.Sqrt, scale=1.0 / (LR * LR)).then_inc(S.sD, 1)
    if home:
        ac.wait_ge(S.sM, 1)
    else:
        ac.wait_ge(S.amv, 4)
    ac.dma_start(T.mo[:], T.mv[:, q, 0:F] if home else T.mvl[:, 0:F]).then_inc(S.stm, 16)
    ac.dma_start(T.vo[:], T.mv[:, q, F:2 * F] if home else T.mvl[:, F:2 * F]).then_inc(S.stm, 16)
    ac.wait_ge(S.stm, 32)

    g.sync.wait_ge(S.sW, 1)
    g.sync.wait_ge(S.a4, len(on) * (L - 1))
    g.sync.dma_start(T.y[:], T.ybuf[:]).then_inc(S.sty, 16)
    g.sync.wait_ge(S.sty, 16)

    g.wait_ge(S.sent, sent[0])
